import numpy as np
import ml_dtypes


def mxq(x, axis, fmt="e4m3"):
    dtype, down = {"e4m3": (ml_dtypes.float8_e4m3fn, 7), "e5m2": (ml_dtypes.float8_e5m2, 14)}[fmt]
    v = np.moveaxis(np.asarray(x, np.float32).astype(ml_dtypes.bfloat16).astype(np.float64), axis, -1)
    blocks = v.reshape(v.shape[:-1] + (-1, 32))
    amax = np.abs(blocks).max(-1, keepdims=True)
    byte = np.maximum(np.where(amax > 0, np.frexp(amax)[1] - 1 + 127, 0) - down, 1)
    scale = np.exp2(byte - 127.0)
    codes = (blocks / scale).astype(np.float32).astype(dtype).astype(np.float64)
    return np.moveaxis((codes * scale).reshape(v.shape), -1, axis)


WIDE = False


def mx_kscale(k, group=512):
    if not WIDE:
        return np.ones(k)
    levels = np.array([18, -18])
    if group != 512:
        return np.exp2(np.random.permutation(np.resize(levels, k // group))).repeat(group)
    if k % 512:
        return np.exp2(np.random.permutation(np.resize(levels, k // 32))).repeat(32)
    a = np.empty((k // 512, 16))
    for p in range(k // 512):
        a[p, :8] = np.random.permutation(np.resize(levels, 8))
        for g in range(8):
            far = levels[np.abs(levels - a[p, g]) >= 10]
            a[p, g + 8] = far[np.random.randint(len(far))]
    return np.exp2(a.ravel()).repeat(32)


def f64(x):
    return np.asarray(x).astype(np.float64)


def silu(v):
    return v / (1.0 + np.exp(-v))


G, D, M, O, N = 4, 128, 128, 128, 512


def sgn(shape):
    return np.random.uniform(0.5, 2.0, shape) * np.where(np.random.standard_normal(shape) < 0, -1.0, 1.0)


def setup_inputs():
    n = np.random.standard_normal
    s_d = mx_kscale(D, 0)
    s_m = mx_kscale(M, 0)
    return {
        "x": (n((G, D, N)) * s_d[:, None]).astype(np.float32),
        "w1": (n((G, D, M)) / np.sqrt(D) / s_d[:, None]).astype(np.float32),
        "w2": (n((G, D, M)) / np.sqrt(D) / s_d[:, None]).astype(np.float32),
        "sh": (np.random.uniform(0.1, 0.4, (G, M, 1))).astype(np.float32),
        "d0": (np.random.uniform(5.0, 9.0, (G, M, N))).astype(np.float32),
        "hs": (sgn((G, M, 1)) * s_m[:, None]).astype(np.float32),
        "wo2": (n((G, M, O)) / np.sqrt(M) / s_m[:, None]).astype(np.float32),
        "res": (0.5 * n((G, O, N))).astype(np.float32),
    }


def reference(x, w1, w2, sh, d0, hs, wo2, res):
    w1q = mxq(f64(w1), 1, "e4m3")
    xq = mxq(f64(x), 1, "e4m3")
    z1 = w1q.transpose(0, 2, 1) @ xq
    w2q = mxq(f64(w2), 1, "e4m3")
    z2 = w2q.transpose(0, 2, 1) @ xq
    q1 = f64(d0) - z1
    h = silu(z2) / (q1 * f64(sh) + 1.0)
    hh = h * f64(hs)
    wo2q = mxq(f64(wo2), 1, "e4m3")
    hhq = mxq(hh, 1, "e4m3")
    y0 = wo2q.transpose(0, 2, 1) @ hhq
    y = y0 + f64(res)
    return y

@@ -1,0 +1,194 @@
+from contextlib import ExitStack
+
+import concourse.mybir as mybir
+
+G, D, M, O, N = 4, 128, 128, 128, 512
+FLOPS = 2 * G * N * (2 * D * M + M * O)
+
+F32 = mybir.dt.float32
+BF16 = mybir.dt.bfloat16
+U32 = mybir.dt.uint32
+U8 = mybir.dt.uint8
+FP8X4 = mybir.dt.float8_e4m3fn_x4
+ACT = mybir.ActivationFunctionType
+ALU = mybir.AluOpType
+
+P = 128
+PACK = 4
+ROWS = 32
+HALVES = 2
+HALF = N // HALVES
+PASS_N = 128
+SPLIT = 160
+
+
+def tile_rows_fkernstudent_kernel(tc, x, w1, w2, sh, d0, hs, wo2, res, out):
+    nc = tc.nc
+    groups = range(G)
+    halves = range(HALVES)
+
+    with ExitStack() as ctx:
+        sb = ctx.enter_context(tc.tile_pool(name="sb", bufs=1))
+        ps = ctx.enter_context(tc.psum_pool(name="ps", bufs=1))
+        ctx.enter_context(tc.manual_schedule())
+
+        def cols(h):
+            return slice(h * HALF, (h + 1) * HALF)
+
+        def load_packed(name, src, width):
+            raw = sb.tile([P, PACK, width], F32, name=name + "_raw")
+            nc.sync.dma_start(out=raw[:], in_=src)
+            return raw
+
+        def words_tile(name, width):
+            return sb.tile([P, width, PACK], BF16, name=name + "_words", align_bytes=64)
+
+        def interleave(copy, words, raw, first, last):
+            copy(out=words[:, first:last, :], in_=raw[:, :, first:last].rearrange("p j c -> p c j"))
+
+        def quantize(name, words, width):
+            codes = sb.tile([P, width], U32, name=name + "_codes", align_bytes=64)
+            scales = sb.tile([P, width], U8, name=name + "_scales", align_bytes=64)
+            nc.vector.quantize_mx(
+                out=codes[:].bitcast(FP8X4), scales=scales[:], in_=words[:].rearrange("p c j -> p (c j)")
+            )
+            return codes, scales
+
+        def product(banks, first_col, weights, moving):
+            for c in range(0, HALF, PASS_N):
+                for g in groups:
+                    rows = slice(ROWS * g, ROWS * (g + 1))
+                    nc.tensor.matmul_mx(
+                        out=banks[g][:, first_col + c : first_col + c + PASS_N],
+                        lhsT=weights[0][rows, :].bitcast(FP8X4),
+                        lhsT_scale=weights[1][rows, :],
+                        rhs=moving[0][rows, c : c + PASS_N].bitcast(FP8X4),
+                        rhs_scale=moving[1][rows, c : c + PASS_N],
+                        start=True,
+                        stop=True,
+                    )
+
+        z2_banks = [ps.tile([P, N], F32, name="z2_bank%d" % g) for g in groups]
+        z1_banks = [ps.tile([P, N], F32, name="z1_bank%d" % g) for g in groups]
+
+        x_rows = x.rearrange("g (p j) n -> (g p) j n", j=PACK)
+        w2_raw = load_packed("w2", w2.rearrange("g (p j) m -> (g p) j m", j=PACK), M)
+        x_raw = [load_packed("x0", x_rows[:, :, cols(0)], HALF)]
+        w1_raw = load_packed("w1", w1.rearrange("g (p j) m -> (g p) j m", j=PACK), M)
+        x_raw.append(load_packed("x1", x_rows[:, :, cols(1)], HALF))
+        d0_sb = [sb.tile([P, 2, N], F32, name="d0_%d" % i) for i in range(2)]
+        sh_sb = sb.tile([P, G], F32)
+        hs_sb = sb.tile([P, G], F32)
+        d0_rows = d0.rearrange("g m n -> m g n")
+        nc.sync.dma_start(out=d0_sb[0][:], in_=d0_rows[:, 0:2, :])
+        nc.sync.dma_start(out=d0_sb[1][:], in_=d0_rows[:, 2:4, :])
+        with nc.allow_non_contiguous_dma(reason="one value a feature"):
+            nc.sync.dma_start(out=sh_sb[:], in_=sh.rearrange("g m o -> m (g o)"))
+            nc.sync.dma_start(out=hs_sb[:], in_=hs.rearrange("g m o -> m (g o)"))
+        wo_raw = load_packed("wo", wo2.rearrange("g (p j) o -> (g p) j o", j=PACK), O)
+        res_sb = sb.tile([P, G, N], F32)
+        nc.sync.dma_start(out=res_sb[:], in_=res.rearrange("g o n -> o g n"))
+
+        w2_words = words_tile("w2", M)
+        w1_words = words_tile("w1", M)
+        x_words = [words_tile("x%d" % h, HALF) for h in halves]
+        gate = [sb.tile([P, G, HALF], F32, name="gate%d" % h) for h in halves]
+
+        def silu_half(h):
+            for g in groups:
+                nc.scalar.activation(out=gate[h][:, g, :], in_=z2_banks[g][:, cols(h)], func=ACT.Silu)
+
+        interleave(nc.vector.tensor_copy, w2_words, w2_raw, 0, M)
+        w2_mx = quantize("w2", w2_words, M)
+        interleave(nc.vector.tensor_copy, x_words[0], x_raw[0], 0, HALF)
+        interleave(nc.scalar.copy, w1_words, w1_raw, 0, M)
+        x0_mx = quantize("x0", x_words[0], HALF)
+        product(z2_banks, 0, w2_mx, x0_mx)
+        silu_half(0)
+        w1_mx = quantize("w1", w1_words, M)
+        product(z1_banks, 0, w1_mx, x0_mx)
+        interleave(nc.vector.tensor_copy, x_words[1], x_raw[1], 0, HALF)
+        x1_mx = quantize("x1", x_words[1], HALF)
+        product(z2_banks, HALF, w2_mx, x1_mx)
+        silu_half(1)
+        product(z1_banks, HALF, w1_mx, x1_mx)
+
+        sh_neg = sb.tile([P, G], F32)
+        root = sb.tile([P, G], F32)
+        sh_sign = sb.tile([P, G], F32)
+        hs_signed = sb.tile([P, G], F32)
+        dist = [sb.tile([P, N], F32, name="dist%d" % g) for g in groups]
+        side = sb.tile([P, G, N], BF16)
+        for g in groups:
+            nc.vector.tensor_tensor(out=dist[g][:], in0=d0_sb[g // 2][:, g % 2, :], in1=z1_banks[g][:], op=ALU.subtract)
+            if g == 1:
+                nc.vector.tensor_scalar(out=sh_neg[:], in0=sh_sb[:], scalar1=0.0, scalar2=-1.0, op0=ALU.add, op1=ALU.mult)
+                nc.vector.tensor_scalar(out=sh_sign[:], in0=sh_sb[:], scalar1=0.0, scalar2=0.5, op0=ALU.is_ge, op1=ALU.subtract)
+            if g == 2:
+                nc.vector.reciprocal(out=root[:], in_=sh_neg[:])
+                nc.vector.scalar_tensor_tensor(out=hs_signed[:], in0=sh_sign[:], scalar=4.0, in1=hs_sb[:], op0=ALU.mult, op1=ALU.mult)
+        wo_words = words_tile("wo", O)
+        interleave(nc.vector.tensor_copy, wo_words, wo_raw, 0, O)
+        for g in groups:
+            nc.vector.tensor_scalar(
+                out=side[:, g, :], in0=dist[g][:], scalar1=root[:, g : g + 1], scalar2=0.5,
+                op0=ALU.is_ge, op1=ALU.subtract,
+            )
+        wo_mx = quantize("wo", wo_words, O)
+
+        inv_root = sb.tile([P, G, N], F32)
+        inv = sb.tile([P, G, N], F32)
+        mag = sb.tile([P, G, N], BF16)
+        hh = [[sb.tile([P, HALF], BF16, name="hh%d_%d" % (h, g)) for g in groups] for h in halves]
+        hh_rows = [sb.tile([P, PACK, HALF], BF16, name="hh_rows%d" % h) for h in halves]
+        pieces = [(h, g) for h in halves for g in groups]
+
+        def inverse_root(h, g):
+            nc.scalar.activation(
+                out=inv_root[:, g, cols(h)], in_=dist[g][:, cols(h)], func=ACT.Abs_reciprocal_sqrt,
+                scale=sh_sb[:, g : g + 1], bias=1.0,
+            )
+
+        def signed(h, g):
+            nc.vector.tensor_tensor(out=hh[h][g][:], in0=mag[:, g, cols(h)], in1=side[:, g, cols(h)], op=ALU.mult)
+            nc.sync.dma_start(out=hh_rows[h][ROWS * g : ROWS * (g + 1), :, :], in_=hh[h][g][:])
+
+        inverse_root(*pieces[0])
+        for i, (h, g) in enumerate(pieces):
+            if i + 1 < len(pieces):
+                inverse_root(*pieces[i + 1])
+            nc.scalar.activation(out=inv[:, g, cols(h)], in_=inv_root[:, g, cols(h)], func=ACT.Square)
+            nc.vector.scalar_tensor_tensor(
+                out=mag[:, g, cols(h)], in0=gate[h][:, g, :], scalar=hs_signed[:, g : g + 1], in1=inv[:, g, cols(h)],
+                op0=ALU.mult, op1=ALU.mult,
+            )
+            if i > 0:
+                signed(*pieces[i - 1])
+        signed(*pieces[-1])
+
+        result = [[sb.tile([P, 2, HALF], F32, name="result%d_%d" % (h, i)) for i in range(2)] for h in halves]
+        out_rows = out.rearrange("g o n -> o g n")
+        hh_words = [words_tile("hh%d" % h, HALF) for h in halves]
+        y_banks = [z2_banks, z1_banks]
+
+        def finish(h, g):
+            nc.vector.tensor_tensor(
+                out=result[h][g // 2][:, g % 2, :], in0=y_banks[h][g][:, 0:HALF], in1=res_sb[:, g, cols(h)], op=ALU.add
+            )
+            if g % 2 == 1:
+                nc.sync.dma_start(out=out_rows[:, g - 1 : g + 1, cols(h)], in_=result[h][g // 2][:])
+
+        interleave(nc.vector.tensor_copy, hh_words[0], hh_rows[0], 0, SPLIT)
+        interleave(nc.scalar.copy, hh_words[0], hh_rows[0], SPLIT, HALF)
+        hh0_mx = quantize("hh0", hh_words[0], HALF)
+        product(y_banks[0], 0, wo_mx, hh0_mx)
+        interleave(nc.scalar.copy, hh_words[1], hh_rows[1], SPLIT, HALF)
+        finish(0, 0)
+        interleave(nc.vector.tensor_copy, hh_words[1], hh_rows[1], 0, SPLIT)
+        finish(0, 1)
+        hh1_mx = quantize("hh1", hh_words[1], HALF)
+        product(y_banks[1], 0, wo_mx, hh1_mx)
+        finish(0, 2)
+        finish(0, 3)
+        for g in groups:
+            finish(1, g)

@@ -16,24 +16,22 @@ ALU = mybir.AluOpType
 P = 128
 PACK = 4
 ROWS = 32
-HALVES = 2
-HALF = N // HALVES
+HALF = N // 2
 PASS_N = 128
-SPLIT = 160
+CHUNKS = [slice(0, 256), slice(256, 384), slice(384, 512)]
+ROW_STEP = 8
 
 
 def tile_rows_fkernstudent_kernel(tc, x, w1, w2, sh, d0, hs, wo2, res, out):
     nc = tc.nc
     groups = range(G)
-    halves = range(HALVES)
+    halves = [slice(0, HALF), slice(HALF, N)]
+    widths = [c.stop - c.start for c in CHUNKS]
 
     with ExitStack() as ctx:
         sb = ctx.enter_context(tc.tile_pool(name="sb", bufs=1))
         ps = ctx.enter_context(tc.psum_pool(name="ps", bufs=1))
         ctx.enter_context(tc.manual_schedule())
-
-        def cols(h):
-            return slice(h * HALF, (h + 1) * HALF)
 
         def load_packed(name, src, width):
             raw = sb.tile([P, PACK, width], F32, name=name + "_raw")
@@ -54,12 +52,12 @@ def tile_rows_fkernstudent_kernel(tc, x, w1, w2, sh, d0, hs, wo2, res, out):
             )
             return codes, scales
 
-        def product(banks, first_col, weights, moving):
-            for c in range(0, HALF, PASS_N):
-                for g in groups:
-                    rows = slice(ROWS * g, ROWS * (g + 1))
+        def product(banks, bank_cols, weights, moving):
+            for g in groups:
+                rows = slice(ROWS * g, ROWS * (g + 1))
+                for c in range(0, bank_cols.stop - bank_cols.start, PASS_N):
                     nc.tensor.matmul_mx(
-                        out=banks[g][:, first_col + c : first_col + c + PASS_N],
+                        out=banks[g][:, bank_cols.start + c : bank_cols.start + c + PASS_N],
                         lhsT=weights[0][rows, :].bitcast(FP8X4),
                         lhsT_scale=weights[1][rows, :],
                         rhs=moving[0][rows, c : c + PASS_N].bitcast(FP8X4),
@@ -71,124 +69,146 @@ def tile_rows_fkernstudent_kernel(tc, x, w1, w2, sh, d0, hs, wo2, res, out):
         z2_banks = [ps.tile([P, N], F32, name="z2_bank%d" % g) for g in groups]
         z1_banks = [ps.tile([P, N], F32, name="z1_bank%d" % g) for g in groups]
 
+        feature_rows = sb.tile([P, ROWS], F32, align_bytes=64)
+        nc.vector.memset(feature_rows[:], 0.0)
+
         x_rows = x.rearrange("g (p j) n -> (g p) j n", j=PACK)
         w2_raw = load_packed("w2", w2.rearrange("g (p j) m -> (g p) j m", j=PACK), M)
-        x_raw = [load_packed("x0", x_rows[:, :, cols(0)], HALF)]
+        x_raw = [load_packed("x%d" % h, x_rows[:, :, cols], HALF) for h, cols in enumerate(halves)]
         w1_raw = load_packed("w1", w1.rearrange("g (p j) m -> (g p) j m", j=PACK), M)
-        x_raw.append(load_packed("x1", x_rows[:, :, cols(1)], HALF))
+        nc.sync.dma_start(out=feature_rows[0:P:ROW_STEP, :], in_=sh.rearrange("g (q i) o -> q g (i o)", i=ROWS))
+        nc.sync.dma_start(out=feature_rows[1:P:ROW_STEP, :], in_=hs.rearrange("g (q i) o -> q g (i o)", i=ROWS))
         d0_sb = [sb.tile([P, 2, N], F32, name="d0_%d" % i) for i in range(2)]
-        sh_sb = sb.tile([P, G], F32)
-        hs_sb = sb.tile([P, G], F32)
         d0_rows = d0.rearrange("g m n -> m g n")
         nc.sync.dma_start(out=d0_sb[0][:], in_=d0_rows[:, 0:2, :])
         nc.sync.dma_start(out=d0_sb[1][:], in_=d0_rows[:, 2:4, :])
-        with nc.allow_non_contiguous_dma(reason="one value a feature"):
-            nc.sync.dma_start(out=sh_sb[:], in_=sh.rearrange("g m o -> m (g o)"))
-            nc.sync.dma_start(out=hs_sb[:], in_=hs.rearrange("g m o -> m (g o)"))
         wo_raw = load_packed("wo", wo2.rearrange("g (p j) o -> (g p) j o", j=PACK), O)
         res_sb = sb.tile([P, G, N], F32)
         nc.sync.dma_start(out=res_sb[:], in_=res.rearrange("g o n -> o g n"))
 
         w2_words = words_tile("w2", M)
         w1_words = words_tile("w1", M)
-        x_words = [words_tile("x%d" % h, HALF) for h in halves]
-        gate = [sb.tile([P, G, HALF], F32, name="gate%d" % h) for h in halves]
+        x_words = [words_tile("x%d" % h, HALF) for h in range(2)]
+        gate = [sb.tile([P, N], F32, name="gate%d" % g) for g in groups]
 
-        def silu_half(h):
+        def silu_half(cols):
             for g in groups:
-                nc.scalar.activation(out=gate[h][:, g, :], in_=z2_banks[g][:, cols(h)], func=ACT.Silu)
+                nc.scalar.activation(out=gate[g][:, cols], in_=z2_banks[g][:, cols], func=ACT.Silu)
 
         interleave(nc.vector.tensor_copy, w2_words, w2_raw, 0, M)
         w2_mx = quantize("w2", w2_words, M)
         interleave(nc.vector.tensor_copy, x_words[0], x_raw[0], 0, HALF)
-        interleave(nc.scalar.copy, w1_words, w1_raw, 0, M)
         x0_mx = quantize("x0", x_words[0], HALF)
-        product(z2_banks, 0, w2_mx, x0_mx)
-        silu_half(0)
-        w1_mx = quantize("w1", w1_words, M)
-        product(z1_banks, 0, w1_mx, x0_mx)
+        product(z2_banks, halves[0], w2_mx, x0_mx)
+        silu_half(halves[0])
         interleave(nc.vector.tensor_copy, x_words[1], x_raw[1], 0, HALF)
+        interleave(nc.vector.tensor_copy, w1_words, w1_raw, 0, M)
         x1_mx = quantize("x1", x_words[1], HALF)
-        product(z2_banks, HALF, w2_mx, x1_mx)
-        silu_half(1)
-        product(z1_banks, HALF, w1_mx, x1_mx)
+        product(z2_banks, halves[1], w2_mx, x1_mx)
+        silu_half(halves[1])
+        w1_mx = quantize("w1", w1_words, M)
+        for g in groups:
+            rows = slice(ROWS * g, ROWS * (g + 1))
+            for c in range(0, N, PASS_N):
+                moving = x0_mx if c < HALF else x1_mx
+                nc.tensor.matmul_mx(
+                    out=z1_banks[g][:, c : c + PASS_N],
+                    lhsT=w1_mx[0][rows, :].bitcast(FP8X4),
+                    lhsT_scale=w1_mx[1][rows, :],
+                    rhs=moving[0][rows, c % HALF : c % HALF + PASS_N].bitcast(FP8X4),
+                    rhs_scale=moving[1][rows, c % HALF : c % HALF + PASS_N],
+                    start=True,
+                    stop=True,
+                )
 
+        features = sb.tile([P, ROWS], F32, align_bytes=64)
+        nc.vector.transpose(out=features[:], in_=feature_rows[:])
+        sh_sb = features[:, 0:ROWS:ROW_STEP]
+        hs_sb = features[:, 1:ROWS:ROW_STEP]
         sh_neg = sb.tile([P, G], F32)
         root = sb.tile([P, G], F32)
         sh_sign = sb.tile([P, G], F32)
         hs_signed = sb.tile([P, G], F32)
         dist = [sb.tile([P, N], F32, name="dist%d" % g) for g in groups]
-        side = sb.tile([P, G, N], BF16)
+        side = [sb.tile([P, N], BF16, name="side%d" % g) for g in groups]
         for g in groups:
             nc.vector.tensor_tensor(out=dist[g][:], in0=d0_sb[g // 2][:, g % 2, :], in1=z1_banks[g][:], op=ALU.subtract)
+            if g == 0:
+                nc.vector.tensor_scalar(out=sh_neg[:], in0=sh_sb, scalar1=0.0, scalar2=-1.0, op0=ALU.add, op1=ALU.mult)
+                nc.vector.tensor_scalar(out=sh_sign[:], in0=sh_sb, scalar1=0.0, scalar2=0.5, op0=ALU.is_ge, op1=ALU.subtract)
             if g == 1:
-                nc.vector.tensor_scalar(out=sh_neg[:], in0=sh_sb[:], scalar1=0.0, scalar2=-1.0, op0=ALU.add, op1=ALU.mult)
-                nc.vector.tensor_scalar(out=sh_sign[:], in0=sh_sb[:], scalar1=0.0, scalar2=0.5, op0=ALU.is_ge, op1=ALU.subtract)
-            if g == 2:
                 nc.vector.reciprocal(out=root[:], in_=sh_neg[:])
-                nc.vector.scalar_tensor_tensor(out=hs_signed[:], in0=sh_sign[:], scalar=4.0, in1=hs_sb[:], op0=ALU.mult, op1=ALU.mult)
-        wo_words = words_tile("wo", O)
-        interleave(nc.vector.tensor_copy, wo_words, wo_raw, 0, O)
+                nc.vector.scalar_tensor_tensor(out=hs_signed[:], in0=sh_sign[:], scalar=4.0, in1=hs_sb, op0=ALU.mult, op1=ALU.mult)
         for g in groups:
             nc.vector.tensor_scalar(
-                out=side[:, g, :], in0=dist[g][:], scalar1=root[:, g : g + 1], scalar2=0.5,
+                out=side[g][:], in0=dist[g][:], scalar1=root[:, g : g + 1], scalar2=0.5,
                 op0=ALU.is_ge, op1=ALU.subtract,
             )
-        wo_mx = quantize("wo", wo_words, O)
+        wo_words = words_tile("wo", O)
+        interleave(nc.vector.tensor_copy, wo_words, wo_raw, 0, O)
 
-        inv_root = sb.tile([P, G, N], F32)
-        inv = sb.tile([P, G, N], F32)
-        mag = sb.tile([P, G, N], BF16)
-        hh = [[sb.tile([P, HALF], BF16, name="hh%d_%d" % (h, g)) for g in groups] for h in halves]
-        hh_rows = [sb.tile([P, PACK, HALF], BF16, name="hh_rows%d" % h) for h in halves]
-        pieces = [(h, g) for h in halves for g in groups]
+        inv_root = [sb.tile([P, N], F32, name="inv_root%d" % g) for g in groups]
+        inv = [sb.tile([P, N], F32, name="inv%d" % g) for g in groups]
+        mag = [sb.tile([P, N], BF16, name="mag%d" % g) for g in groups]
+        hh = [sb.tile([P, N], BF16, name="hh%d" % g) for g in groups]
+        hh_rows = [sb.tile([P, PACK, w], BF16, name="hh_rows%d" % c) for c, w in enumerate(widths)]
+        pieces = [(c, g) for c in range(len(CHUNKS)) for g in groups]
 
-        def inverse_root(h, g):
+        def inverse_root(c, g):
             nc.scalar.activation(
-                out=inv_root[:, g, cols(h)], in_=dist[g][:, cols(h)], func=ACT.Abs_reciprocal_sqrt,
-                scale=sh_sb[:, g : g + 1], bias=1.0,
+                out=inv_root[g][:, CHUNKS[c]], in_=dist[g][:, CHUNKS[c]], func=ACT.Abs_reciprocal_sqrt,
+                scale=features[:, ROW_STEP * g : ROW_STEP * g + 1], bias=1.0,
             )
 
-        def signed(h, g):
-            nc.vector.tensor_tensor(out=hh[h][g][:], in0=mag[:, g, cols(h)], in1=side[:, g, cols(h)], op=ALU.mult)
-            nc.sync.dma_start(out=hh_rows[h][ROWS * g : ROWS * (g + 1), :, :], in_=hh[h][g][:])
+        def signed(c, g):
+            cols = CHUNKS[c]
+            nc.vector.tensor_tensor(out=hh[g][:, cols], in0=mag[g][:, cols], in1=side[g][:, cols], op=ALU.mult)
+            nc.sync.dma_start(out=hh_rows[c][ROWS * g : ROWS * (g + 1), :, :], in_=hh[g][:, cols])
 
         inverse_root(*pieces[0])
-        for i, (h, g) in enumerate(pieces):
+        for i, (c, g) in enumerate(pieces):
+            cols = CHUNKS[c]
             if i + 1 < len(pieces):
                 inverse_root(*pieces[i + 1])
-            nc.scalar.activation(out=inv[:, g, cols(h)], in_=inv_root[:, g, cols(h)], func=ACT.Square)
+            nc.scalar.activation(out=inv[g][:, cols], in_=inv_root[g][:, cols], func=ACT.Square)
             nc.vector.scalar_tensor_tensor(
-                out=mag[:, g, cols(h)], in0=gate[h][:, g, :], scalar=hs_signed[:, g : g + 1], in1=inv[:, g, cols(h)],
+                out=mag[g][:, cols], in0=gate[g][:, cols], scalar=hs_signed[:, g : g + 1], in1=inv[g][:, cols],
                 op0=ALU.mult, op1=ALU.mult,
             )
-            if i > 0:
+            if i == 0:
+                wo_mx = quantize("wo", wo_words, O)
+            else:
                 signed(*pieces[i - 1])
         signed(*pieces[-1])
 
-        result = [[sb.tile([P, 2, HALF], F32, name="result%d_%d" % (h, i)) for i in range(2)] for h in halves]
+        result = [[sb.tile([P, 2, w], F32, name="result%d_%d" % (c, i)) for i in range(2)] for c, w in enumerate(widths)]
         out_rows = out.rearrange("g o n -> o g n")
-        hh_words = [words_tile("hh%d" % h, HALF) for h in halves]
-        y_banks = [z2_banks, z1_banks]
+        hh_words = [words_tile("hh%d" % c, w) for c, w in enumerate(widths)]
+        y_banks = [z2_banks, z1_banks, z2_banks]
 
-        def finish(h, g):
+        def second_layer(c):
+            product(y_banks[c], CHUNKS[c], wo_mx, quantize("hh%d" % c, hh_words[c], widths[c]))
+
+        def finish(c, g):
+            cols = CHUNKS[c]
             nc.vector.tensor_tensor(
-                out=result[h][g // 2][:, g % 2, :], in0=y_banks[h][g][:, 0:HALF], in1=res_sb[:, g, cols(h)], op=ALU.add
+                out=result[c][g // 2][:, g % 2, :], in0=y_banks[c][g][:, cols], in1=res_sb[:, g, cols], op=ALU.add
             )
             if g % 2 == 1:
-                nc.sync.dma_start(out=out_rows[:, g - 1 : g + 1, cols(h)], in_=result[h][g // 2][:])
+                nc.sync.dma_start(out=out_rows[:, g - 1 : g + 1, cols], in_=result[c][g // 2][:])
 
-        interleave(nc.vector.tensor_copy, hh_words[0], hh_rows[0], 0, SPLIT)
-        interleave(nc.scalar.copy, hh_words[0], hh_rows[0], SPLIT, HALF)
-        hh0_mx = quantize("hh0", hh_words[0], HALF)
-        product(y_banks[0], 0, wo_mx, hh0_mx)
-        interleave(nc.scalar.copy, hh_words[1], hh_rows[1], SPLIT, HALF)
+        interleave(nc.scalar.copy, hh_words[0], hh_rows[0], 0, 128)
+        interleave(nc.vector.tensor_copy, hh_words[0], hh_rows[0], 128, 256)
+        second_layer(0)
+        interleave(nc.scalar.copy, hh_words[1], hh_rows[1], 0, widths[1])
+        interleave(nc.scalar.copy, hh_words[2], hh_rows[2], 0, widths[2])
         finish(0, 0)
-        interleave(nc.vector.tensor_copy, hh_words[1], hh_rows[1], 0, SPLIT)
+        second_layer(1)
         finish(0, 1)
-        hh1_mx = quantize("hh1", hh_words[1], HALF)
-        product(y_banks[1], 0, wo_mx, hh1_mx)
         finish(0, 2)
         finish(0, 3)
+        second_layer(2)
         for g in groups:
             finish(1, g)
+        for g in groups:
+            finish(2, g)

@@ -1,3 +1,4 @@
+import itertools
 from contextlib import ExitStack
 
 import concourse.mybir as mybir
@@ -16,55 +17,61 @@ ALU = mybir.AluOpType
 P = 128
 PACK = 4
 ROWS = 32
-HALF = N // 2
 PASS_N = 128
-CHUNKS = [slice(0, 256), slice(256, 384), slice(384, 512)]
-ROW_STEP = 8
+RUN = 4
+ROW_STEP = ROWS // G
+GROUP_PAIRS = ((0, 1), (2, 3))
+
+HALF = N // 2
+HALVES = (slice(0, HALF), slice(HALF, N))
+CHUNKS = (slice(0, HALF), slice(HALF, HALF + PASS_N), slice(HALF + PASS_N, N))
+SCALAR_COLS = 96
 
 
 def tile_rows_fkernstudent_kernel(tc, x, w1, w2, sh, d0, hs, wo2, res, out):
     nc = tc.nc
     groups = range(G)
-    halves = [slice(0, HALF), slice(HALF, N)]
-    widths = [c.stop - c.start for c in CHUNKS]
+    widths = [cols.stop - cols.start for cols in CHUNKS]
 
     with ExitStack() as ctx:
         sb = ctx.enter_context(tc.tile_pool(name="sb", bufs=1))
         ps = ctx.enter_context(tc.psum_pool(name="ps", bufs=1))
         ctx.enter_context(tc.manual_schedule())
 
-        def load_packed(name, src, width):
-            raw = sb.tile([P, PACK, width], F32, name=name + "_raw")
-            nc.sync.dma_start(out=raw[:], in_=src)
+        def load_packed(name, src, cols):
+            raw = sb.tile([P, PACK, cols.stop - cols.start], F32, name=name + "_raw")
+            nc.sync.dma_start(out=raw[:], in_=src.rearrange("g (p j) c -> (g p) j c", j=PACK)[:, :, cols])
             return raw
 
-        def words_tile(name, width):
-            return sb.tile([P, width, PACK], BF16, name=name + "_words", align_bytes=64)
+        def grouped_tile(name, width):
+            return sb.tile([P, width, PACK], BF16, name=name + "_grouped", align_bytes=64)
 
-        def interleave(copy, words, raw, first, last):
-            copy(out=words[:, first:last, :], in_=raw[:, :, first:last].rearrange("p j c -> p c j"))
+        def interleave(copy, grouped, raw, cols):
+            copy(
+                out=grouped[:, cols, :].rearrange("p (c i) j -> p c j i", i=RUN),
+                in_=raw[:, :, cols].rearrange("p j (c i) -> p c j i", i=RUN),
+            )
 
-        def quantize(name, words, width):
+        def quantize(name, grouped, width):
             codes = sb.tile([P, width], U32, name=name + "_codes", align_bytes=64)
             scales = sb.tile([P, width], U8, name=name + "_scales", align_bytes=64)
             nc.vector.quantize_mx(
-                out=codes[:].bitcast(FP8X4), scales=scales[:], in_=words[:].rearrange("p c j -> p (c j)")
+                out=codes[:].bitcast(FP8X4), scales=scales[:], in_=grouped[:].rearrange("p c j -> p (c j)")
             )
             return codes, scales
 
-        def product(banks, bank_cols, weights, moving):
-            for g in groups:
+        def product(banks, cols, weights, moving, some_groups):
+            for first, g in itertools.product(range(0, cols.stop - cols.start, PASS_N), some_groups):
                 rows = slice(ROWS * g, ROWS * (g + 1))
-                for c in range(0, bank_cols.stop - bank_cols.start, PASS_N):
-                    nc.tensor.matmul_mx(
-                        out=banks[g][:, bank_cols.start + c : bank_cols.start + c + PASS_N],
-                        lhsT=weights[0][rows, :].bitcast(FP8X4),
-                        lhsT_scale=weights[1][rows, :],
-                        rhs=moving[0][rows, c : c + PASS_N].bitcast(FP8X4),
-                        rhs_scale=moving[1][rows, c : c + PASS_N],
-                        start=True,
-                        stop=True,
-                    )
+                nc.tensor.matmul_mx(
+                    out=banks[g][:, cols.start + first : cols.start + first + PASS_N],
+                    lhsT=weights[0][rows, :].bitcast(FP8X4),
+                    lhsT_scale=weights[1][rows, :],
+                    rhs=moving[0][rows, first : first + PASS_N].bitcast(FP8X4),
+                    rhs_scale=moving[1][rows, first : first + PASS_N],
+                    start=True,
+                    stop=True,
+                )
 
         z2_banks = [ps.tile([P, N], F32, name="z2_bank%d" % g) for g in groups]
         z1_banks = [ps.tile([P, N], F32, name="z1_bank%d" % g) for g in groups]
@@ -72,86 +79,83 @@ def tile_rows_fkernstudent_kernel(tc, x, w1, w2, sh, d0, hs, wo2, res, out):
         feature_rows = sb.tile([P, ROWS], F32, align_bytes=64)
         nc.vector.memset(feature_rows[:], 0.0)
 
-        x_rows = x.rearrange("g (p j) n -> (g p) j n", j=PACK)
-        w2_raw = load_packed("w2", w2.rearrange("g (p j) m -> (g p) j m", j=PACK), M)
-        x_raw = [load_packed("x%d" % h, x_rows[:, :, cols], HALF) for h, cols in enumerate(halves)]
-        w1_raw = load_packed("w1", w1.rearrange("g (p j) m -> (g p) j m", j=PACK), M)
+        x0_raw = load_packed("x0", x, HALVES[0])
+        w2_raw = load_packed("w2", w2, slice(0, M))
+        x1_raw = load_packed("x1", x, HALVES[1])
+        w1_raw = load_packed("w1", w1, slice(0, M))
         nc.sync.dma_start(out=feature_rows[0:P:ROW_STEP, :], in_=sh.rearrange("g (q i) o -> q g (i o)", i=ROWS))
         nc.sync.dma_start(out=feature_rows[1:P:ROW_STEP, :], in_=hs.rearrange("g (q i) o -> q g (i o)", i=ROWS))
-        d0_sb = [sb.tile([P, 2, N], F32, name="d0_%d" % i) for i in range(2)]
-        d0_rows = d0.rearrange("g m n -> m g n")
-        nc.sync.dma_start(out=d0_sb[0][:], in_=d0_rows[:, 0:2, :])
-        nc.sync.dma_start(out=d0_sb[1][:], in_=d0_rows[:, 2:4, :])
-        wo_raw = load_packed("wo", wo2.rearrange("g (p j) o -> (g p) j o", j=PACK), O)
+        d0_sb = [sb.tile([P, N], F32, name="d0_%d" % g) for g in groups]
+        nc.sync.dma_start(out=d0_sb[0][:], in_=d0[0])
+        wo_raw = load_packed("wo", wo2, slice(0, O))
+        for g in range(1, G):
+            nc.sync.dma_start(out=d0_sb[g][:], in_=d0[g])
         res_sb = sb.tile([P, G, N], F32)
         nc.sync.dma_start(out=res_sb[:], in_=res.rearrange("g o n -> o g n"))
 
-        w2_words = words_tile("w2", M)
-        w1_words = words_tile("w1", M)
-        x_words = [words_tile("x%d" % h, HALF) for h in range(2)]
         gate = [sb.tile([P, N], F32, name="gate%d" % g) for g in groups]
 
-        def silu_half(cols):
+        def gate_half(cols, x_mx):
+            for pair in GROUP_PAIRS:
+                product(z2_banks, cols, w2_mx, x_mx, pair)
             for g in groups:
                 nc.scalar.activation(out=gate[g][:, cols], in_=z2_banks[g][:, cols], func=ACT.Silu)
 
-        interleave(nc.vector.tensor_copy, w2_words, w2_raw, 0, M)
-        w2_mx = quantize("w2", w2_words, M)
-        interleave(nc.vector.tensor_copy, x_words[0], x_raw[0], 0, HALF)
-        x0_mx = quantize("x0", x_words[0], HALF)
-        product(z2_banks, halves[0], w2_mx, x0_mx)
-        silu_half(halves[0])
-        interleave(nc.vector.tensor_copy, x_words[1], x_raw[1], 0, HALF)
-        interleave(nc.vector.tensor_copy, w1_words, w1_raw, 0, M)
-        x1_mx = quantize("x1", x_words[1], HALF)
-        product(z2_banks, halves[1], w2_mx, x1_mx)
-        silu_half(halves[1])
-        w1_mx = quantize("w1", w1_words, M)
-        for g in groups:
-            rows = slice(ROWS * g, ROWS * (g + 1))
-            for c in range(0, N, PASS_N):
-                moving = x0_mx if c < HALF else x1_mx
-                nc.tensor.matmul_mx(
-                    out=z1_banks[g][:, c : c + PASS_N],
-                    lhsT=w1_mx[0][rows, :].bitcast(FP8X4),
-                    lhsT_scale=w1_mx[1][rows, :],
-                    rhs=moving[0][rows, c % HALF : c % HALF + PASS_N].bitcast(FP8X4),
-                    rhs_scale=moving[1][rows, c % HALF : c % HALF + PASS_N],
-                    start=True,
-                    stop=True,
-                )
+        x0_grouped = grouped_tile("x0", HALF)
+        w2_grouped = grouped_tile("w2", M)
+        interleave(nc.vector.tensor_copy, x0_grouped, x0_raw, slice(0, HALF))
+        interleave(nc.vector.tensor_copy, w2_grouped, w2_raw, slice(0, M))
+        x0_mx = quantize("x0", x0_grouped, HALF)
+        w2_mx = quantize("w2", w2_grouped, M)
+        gate_half(HALVES[0], x0_mx)
 
+        x1_grouped = grouped_tile("x1", HALF)
         features = sb.tile([P, ROWS], F32, align_bytes=64)
+        interleave(nc.vector.tensor_copy, x1_grouped, x1_raw, slice(0, HALF))
         nc.vector.transpose(out=features[:], in_=feature_rows[:])
-        sh_sb = features[:, 0:ROWS:ROW_STEP]
-        hs_sb = features[:, 1:ROWS:ROW_STEP]
-        sh_neg = sb.tile([P, G], F32)
-        root = sb.tile([P, G], F32)
-        sh_sign = sb.tile([P, G], F32)
-        hs_signed = sb.tile([P, G], F32)
+        x1_mx = quantize("x1", x1_grouped, HALF)
+        gate_half(HALVES[1], x1_mx)
+
+        sh_cols = features[:, 0:ROWS:ROW_STEP]
+        hs_cols = features[:, 1:ROWS:ROW_STEP]
+        minus_sh = sb.tile([P, G], F32)
+        half_sign_sh = sb.tile([P, G], F32)
+        w1_grouped = grouped_tile("w1", M)
+        interleave(nc.vector.tensor_copy, w1_grouped, w1_raw, slice(0, M))
+        nc.vector.tensor_scalar(out=minus_sh[:], in0=sh_cols, scalar1=0.0, scalar2=-1.0, op0=ALU.add, op1=ALU.mult)
+        nc.vector.tensor_scalar(
+            out=half_sign_sh[:], in0=sh_cols, scalar1=0.0, scalar2=0.5, op0=ALU.is_ge, op1=ALU.subtract
+        )
+        w1_mx = quantize("w1", w1_grouped, M)
+        for pair in GROUP_PAIRS:
+            product(z1_banks, HALVES[0], w1_mx, x0_mx, pair)
+            product(z1_banks, HALVES[1], w1_mx, x1_mx, pair)
+
+        zero_at = sb.tile([P, G], F32)
+        signed_hs = sb.tile([P, G], F32)
+        wo_grouped = grouped_tile("wo", O)
+        interleave(nc.vector.tensor_copy, wo_grouped, wo_raw, slice(0, O))
+        nc.vector.reciprocal(out=zero_at[:], in_=minus_sh[:])
+        nc.vector.scalar_tensor_tensor(
+            out=signed_hs[:], in0=half_sign_sh[:], scalar=4.0, in1=hs_cols, op0=ALU.mult, op1=ALU.mult
+        )
+        wo_mx = quantize("wo", wo_grouped, O)
+
         dist = [sb.tile([P, N], F32, name="dist%d" % g) for g in groups]
         side = [sb.tile([P, N], BF16, name="side%d" % g) for g in groups]
         for g in groups:
-            nc.vector.tensor_tensor(out=dist[g][:], in0=d0_sb[g // 2][:, g % 2, :], in1=z1_banks[g][:], op=ALU.subtract)
-            if g == 0:
-                nc.vector.tensor_scalar(out=sh_neg[:], in0=sh_sb, scalar1=0.0, scalar2=-1.0, op0=ALU.add, op1=ALU.mult)
-                nc.vector.tensor_scalar(out=sh_sign[:], in0=sh_sb, scalar1=0.0, scalar2=0.5, op0=ALU.is_ge, op1=ALU.subtract)
-            if g == 1:
-                nc.vector.reciprocal(out=root[:], in_=sh_neg[:])
-                nc.vector.scalar_tensor_tensor(out=hs_signed[:], in0=sh_sign[:], scalar=4.0, in1=hs_sb, op0=ALU.mult, op1=ALU.mult)
+            nc.vector.tensor_tensor(out=dist[g][:], in0=d0_sb[g][:], in1=z1_banks[g][:], op=ALU.subtract)
         for g in groups:
             nc.vector.tensor_scalar(
-                out=side[g][:], in0=dist[g][:], scalar1=root[:, g : g + 1], scalar2=0.5,
+                out=side[g][:], in0=dist[g][:], scalar1=zero_at[:, g : g + 1], scalar2=0.5,
                 op0=ALU.is_ge, op1=ALU.subtract,
             )
-        wo_words = words_tile("wo", O)
-        interleave(nc.vector.tensor_copy, wo_words, wo_raw, 0, O)
 
         inv_root = [sb.tile([P, N], F32, name="inv_root%d" % g) for g in groups]
-        inv = [sb.tile([P, N], F32, name="inv%d" % g) for g in groups]
-        mag = [sb.tile([P, N], BF16, name="mag%d" % g) for g in groups]
+        inv_abs = [sb.tile([P, N], F32, name="inv_abs%d" % g) for g in groups]
+        unsigned = [sb.tile([P, N], BF16, name="unsigned%d" % g) for g in groups]
         hh = [sb.tile([P, N], BF16, name="hh%d" % g) for g in groups]
-        hh_rows = [sb.tile([P, PACK, w], BF16, name="hh_rows%d" % c) for c, w in enumerate(widths)]
+        hh_raw = [sb.tile([P, PACK, width], BF16, name="hh%d_raw" % c) for c, width in enumerate(widths)]
         pieces = [(c, g) for c in range(len(CHUNKS)) for g in groups]
 
         def inverse_root(c, g):
@@ -160,55 +164,56 @@ def tile_rows_fkernstudent_kernel(tc, x, w1, w2, sh, d0, hs, wo2, res, out):
                 scale=features[:, ROW_STEP * g : ROW_STEP * g + 1], bias=1.0,
             )
 
-        def signed(c, g):
+        def sign_and_move(c, g):
             cols = CHUNKS[c]
-            nc.vector.tensor_tensor(out=hh[g][:, cols], in0=mag[g][:, cols], in1=side[g][:, cols], op=ALU.mult)
-            nc.sync.dma_start(out=hh_rows[c][ROWS * g : ROWS * (g + 1), :, :], in_=hh[g][:, cols])
+            nc.vector.tensor_tensor(out=hh[g][:, cols], in0=unsigned[g][:, cols], in1=side[g][:, cols], op=ALU.mult)
+            nc.sync.dma_start(out=hh_raw[c][ROWS * g : ROWS * (g + 1), :, :], in_=hh[g][:, cols])
 
         inverse_root(*pieces[0])
         for i, (c, g) in enumerate(pieces):
             cols = CHUNKS[c]
             if i + 1 < len(pieces):
                 inverse_root(*pieces[i + 1])
-            nc.scalar.activation(out=inv[g][:, cols], in_=inv_root[g][:, cols], func=ACT.Square)
+            nc.scalar.activation(out=inv_abs[g][:, cols], in_=inv_root[g][:, cols], func=ACT.Square)
             nc.vector.scalar_tensor_tensor(
-                out=mag[g][:, cols], in0=gate[g][:, cols], scalar=hs_signed[:, g : g + 1], in1=inv[g][:, cols],
-                op0=ALU.mult, op1=ALU.mult,
+                out=unsigned[g][:, cols], in0=gate[g][:, cols], scalar=signed_hs[:, g : g + 1],
+                in1=inv_abs[g][:, cols], op0=ALU.mult, op1=ALU.mult,
             )
-            if i == 0:
-                wo_mx = quantize("wo", wo_words, O)
-            else:
-                signed(*pieces[i - 1])
-        signed(*pieces[-1])
+            if i > 0:
+                sign_and_move(*pieces[i - 1])
+        sign_and_move(*pieces[-1])
 
-        result = [[sb.tile([P, 2, w], F32, name="result%d_%d" % (c, i)) for i in range(2)] for c, w in enumerate(widths)]
-        out_rows = out.rearrange("g o n -> o g n")
-        hh_words = [words_tile("hh%d" % c, w) for c, w in enumerate(widths)]
         y_banks = [z2_banks, z1_banks, z2_banks]
+        hh_grouped = [grouped_tile("hh%d" % c, width) for c, width in enumerate(widths)]
+        result = [
+            [sb.tile([P, len(pair), width], F32, name="result%d_%d" % (c, pair[0])) for pair in GROUP_PAIRS]
+            for c, width in enumerate(widths)
+        ]
+        out_rows = out.rearrange("g o n -> o g n")
 
         def second_layer(c):
-            product(y_banks[c], CHUNKS[c], wo_mx, quantize("hh%d" % c, hh_words[c], widths[c]))
+            hh_mx = quantize("hh%d" % c, hh_grouped[c], widths[c])
+            for pair in GROUP_PAIRS:
+                product(y_banks[c], CHUNKS[c], wo_mx, hh_mx, pair)
 
-        def finish(c, g):
+        def add_residual(c, some_groups):
             cols = CHUNKS[c]
-            nc.vector.tensor_tensor(
-                out=result[c][g // 2][:, g % 2, :], in0=y_banks[c][g][:, cols], in1=res_sb[:, g, cols], op=ALU.add
-            )
-            if g % 2 == 1:
-                nc.sync.dma_start(out=out_rows[:, g - 1 : g + 1, cols], in_=result[c][g // 2][:])
+            for g in some_groups:
+                pair_result = result[c][g // 2]
+                nc.vector.tensor_tensor(
+                    out=pair_result[:, g % 2, :], in0=y_banks[c][g][:, cols], in1=res_sb[:, g, cols], op=ALU.add
+                )
+                if g % 2 == 1:
+                    nc.sync.dma_start(out=out_rows[:, g - 1 : g + 1, cols], in_=pair_result[:])
 
-        interleave(nc.scalar.copy, hh_words[0], hh_rows[0], 0, 128)
-        interleave(nc.vector.tensor_copy, hh_words[0], hh_rows[0], 128, 256)
+        interleave(nc.scalar.copy, hh_grouped[0], hh_raw[0], slice(0, SCALAR_COLS))
+        interleave(nc.vector.tensor_copy, hh_grouped[0], hh_raw[0], slice(SCALAR_COLS, widths[0]))
         second_layer(0)
-        interleave(nc.scalar.copy, hh_words[1], hh_rows[1], 0, widths[1])
-        interleave(nc.scalar.copy, hh_words[2], hh_rows[2], 0, widths[2])
-        finish(0, 0)
+        interleave(nc.scalar.copy, hh_grouped[1], hh_raw[1], slice(0, widths[1]))
+        interleave(nc.scalar.copy, hh_grouped[2], hh_raw[2], slice(0, widths[2]))
+        add_residual(0, range(0, 1))
         second_layer(1)
-        finish(0, 1)
-        finish(0, 2)
-        finish(0, 3)
+        add_residual(0, range(1, G))
         second_layer(2)
-        for g in groups:
-            finish(1, g)
-        for g in groups:
-            finish(2, g)
+        add_residual(1, groups)
+        add_residual(2, groups)

import itertools
from contextlib import ExitStack

import concourse.mybir as mybir

G, D, M, O, N = 4, 128, 128, 128, 512
FLOPS = 2 * G * N * (2 * D * M + M * O)

F32 = mybir.dt.float32
BF16 = mybir.dt.bfloat16
U32 = mybir.dt.uint32
U8 = mybir.dt.uint8
FP8X4 = mybir.dt.float8_e4m3fn_x4
ACT = mybir.ActivationFunctionType
ALU = mybir.AluOpType

P = 128
PACK = 4
ROWS = 32
PASS_N = 128
RUN = 4
ROW_STEP = ROWS // G
GROUP_PAIRS = ((0, 1), (2, 3))

HALF = N // 2
HALVES = (slice(0, HALF), slice(HALF, N))
CHUNKS = (slice(0, HALF), slice(HALF, HALF + PASS_N), slice(HALF + PASS_N, N))
SCALAR_COLS = 96


def tile_rows_fkernstudent_kernel(tc, x, w1, w2, sh, d0, hs, wo2, res, out):
    nc = tc.nc
    groups = range(G)
    widths = [cols.stop - cols.start for cols in CHUNKS]

    with ExitStack() as ctx:
        sb = ctx.enter_context(tc.tile_pool(name="sb", bufs=1))
        ps = ctx.enter_context(tc.psum_pool(name="ps", bufs=1))
        ctx.enter_context(tc.manual_schedule())

        def load_packed(name, src, cols):
            raw = sb.tile([P, PACK, cols.stop - cols.start], F32, name=name + "_raw")
            nc.sync.dma_start(out=raw[:], in_=src.rearrange("g (p j) c -> (g p) j c", j=PACK)[:, :, cols])
            return raw

        def grouped_tile(name, width):
            return sb.tile([P, width, PACK], BF16, name=name + "_grouped", align_bytes=64)

        def interleave(copy, grouped, raw, cols):
            copy(
                out=grouped[:, cols, :].rearrange("p (c i) j -> p c j i", i=RUN),
                in_=raw[:, :, cols].rearrange("p j (c i) -> p c j i", i=RUN),
            )

        def quantize(name, grouped, width):
            codes = sb.tile([P, width], U32, name=name + "_codes", align_bytes=64)
            scales = sb.tile([P, width], U8, name=name + "_scales", align_bytes=64)
            nc.vector.quantize_mx(
                out=codes[:].bitcast(FP8X4), scales=scales[:], in_=grouped[:].rearrange("p c j -> p (c j)")
            )
            return codes, scales

        def product(banks, cols, weights, moving, some_groups):
            for first, g in itertools.product(range(0, cols.stop - cols.start, PASS_N), some_groups):
                rows = slice(ROWS * g, ROWS * (g + 1))
                nc.tensor.matmul_mx(
                    out=banks[g][:, cols.start + first : cols.start + first + PASS_N],
                    lhsT=weights[0][rows, :].bitcast(FP8X4),
                    lhsT_scale=weights[1][rows, :],
                    rhs=moving[0][rows, first : first + PASS_N].bitcast(FP8X4),
                    rhs_scale=moving[1][rows, first : first + PASS_N],
                    start=True,
                    stop=True,
                )

        z2_banks = [ps.tile([P, N], F32, name="z2_bank%d" % g) for g in groups]
        z1_banks = [ps.tile([P, N], F32, name="z1_bank%d" % g) for g in groups]

        feature_rows = sb.tile([P, ROWS], F32, align_bytes=64)
        nc.vector.memset(feature_rows[:], 0.0)

        x0_raw = load_packed("x0", x, HALVES[0])
        w2_raw = load_packed("w2", w2, slice(0, M))
        x1_raw = load_packed("x1", x, HALVES[1])
        w1_raw = load_packed("w1", w1, slice(0, M))
        nc.sync.dma_start(out=feature_rows[0:P:ROW_STEP, :], in_=sh.rearrange("g (q i) o -> q g (i o)", i=ROWS))
        nc.sync.dma_start(out=feature_rows[1:P:ROW_STEP, :], in_=hs.rearrange("g (q i) o -> q g (i o)", i=ROWS))
        d0_sb = [sb.tile([P, N], F32, name="d0_%d" % g) for g in groups]
        nc.sync.dma_start(out=d0_sb[0][:], in_=d0[0])
        wo_raw = load_packed("wo", wo2, slice(0, O))
        for g in range(1, G):
            nc.sync.dma_start(out=d0_sb[g][:], in_=d0[g])
        res_sb = sb.tile([P, G, N], F32)
        nc.sync.dma_start(out=res_sb[:], in_=res.rearrange("g o n -> o g n"))

        gate = [sb.tile([P, N], F32, name="gate%d" % g) for g in groups]

        def gate_half(cols, x_mx):
            for pair in GROUP_PAIRS:
                product(z2_banks, cols, w2_mx, x_mx, pair)
            for g in groups:
                nc.scalar.activation(out=gate[g][:, cols], in_=z2_banks[g][:, cols], func=ACT.Silu)

        x0_grouped = grouped_tile("x0", HALF)
        w2_grouped = grouped_tile("w2", M)
        interleave(nc.vector.tensor_copy, x0_grouped, x0_raw, slice(0, HALF))
        interleave(nc.vector.tensor_copy, w2_grouped, w2_raw, slice(0, M))
        x0_mx = quantize("x0", x0_grouped, HALF)
        w2_mx = quantize("w2", w2_grouped, M)
        gate_half(HALVES[0], x0_mx)

        x1_grouped = grouped_tile("x1", HALF)
        features = sb.tile([P, ROWS], F32, align_bytes=64)
        interleave(nc.vector.tensor_copy, x1_grouped, x1_raw, slice(0, HALF))
        nc.vector.transpose(out=features[:], in_=feature_rows[:])
        x1_mx = quantize("x1", x1_grouped, HALF)
        gate_half(HALVES[1], x1_mx)

        sh_cols = features[:, 0:ROWS:ROW_STEP]
        hs_cols = features[:, 1:ROWS:ROW_STEP]
        minus_sh = sb.tile([P, G], F32)
        half_sign_sh = sb.tile([P, G], F32)
        w1_grouped = grouped_tile("w1", M)
        interleave(nc.vector.tensor_copy, w1_grouped, w1_raw, slice(0, M))
        nc.vector.tensor_scalar(out=minus_sh[:], in0=sh_cols, scalar1=0.0, scalar2=-1.0, op0=ALU.add, op1=ALU.mult)
        nc.vector.tensor_scalar(
            out=half_sign_sh[:], in0=sh_cols, scalar1=0.0, scalar2=0.5, op0=ALU.is_ge, op1=ALU.subtract
        )
        w1_mx = quantize("w1", w1_grouped, M)
        for pair in GROUP_PAIRS:
            product(z1_banks, HALVES[0], w1_mx, x0_mx, pair)
            product(z1_banks, HALVES[1], w1_mx, x1_mx, pair)

        zero_at = sb.tile([P, G], F32)
        signed_hs = sb.tile([P, G], F32)
        wo_grouped = grouped_tile("wo", O)
        interleave(nc.vector.tensor_copy, wo_grouped, wo_raw, slice(0, O))
        nc.vector.reciprocal(out=zero_at[:], in_=minus_sh[:])
        nc.vector.scalar_tensor_tensor(
            out=signed_hs[:], in0=half_sign_sh[:], scalar=4.0, in1=hs_cols, op0=ALU.mult, op1=ALU.mult
        )
        wo_mx = quantize("wo", wo_grouped, O)

        dist = [sb.tile([P, N], F32, name="dist%d" % g) for g in groups]
        side = [sb.tile([P, N], BF16, name="side%d" % g) for g in groups]
        for g in groups:
            nc.vector.tensor_tensor(out=dist[g][:], in0=d0_sb[g][:], in1=z1_banks[g][:], op=ALU.subtract)
        for g in groups:
            nc.vector.tensor_scalar(
                out=side[g][:], in0=dist[g][:], scalar1=zero_at[:, g : g + 1], scalar2=0.5,
                op0=ALU.is_ge, op1=ALU.subtract,
            )

        inv_root = [sb.tile([P, N], F32, name="inv_root%d" % g) for g in groups]
        inv_abs = [sb.tile([P, N], F32, name="inv_abs%d" % g) for g in groups]
        unsigned = [sb.tile([P, N], BF16, name="unsigned%d" % g) for g in groups]
        hh = [sb.tile([P, N], BF16, name="hh%d" % g) for g in groups]
        hh_raw = [sb.tile([P, PACK, width], BF16, name="hh%d_raw" % c) for c, width in enumerate(widths)]
        pieces = [(c, g) for c in range(len(CHUNKS)) for g in groups]

        def inverse_root(c, g):
            nc.scalar.activation(
                out=inv_root[g][:, CHUNKS[c]], in_=dist[g][:, CHUNKS[c]], func=ACT.Abs_reciprocal_sqrt,
                scale=features[:, ROW_STEP * g : ROW_STEP * g + 1], bias=1.0,
            )

        def sign_and_move(c, g):
            cols = CHUNKS[c]
            nc.vector.tensor_tensor(out=hh[g][:, cols], in0=unsigned[g][:, cols], in1=side[g][:, cols], op=ALU.mult)
            nc.sync.dma_start(out=hh_raw[c][ROWS * g : ROWS * (g + 1), :, :], in_=hh[g][:, cols])

        inverse_root(*pieces[0])
        for i, (c, g) in enumerate(pieces):
            cols = CHUNKS[c]
            if i + 1 < len(pieces):
                inverse_root(*pieces[i + 1])
            nc.scalar.activation(out=inv_abs[g][:, cols], in_=inv_root[g][:, cols], func=ACT.Square)
            nc.vector.scalar_tensor_tensor(
                out=unsigned[g][:, cols], in0=gate[g][:, cols], scalar=signed_hs[:, g : g + 1],
                in1=inv_abs[g][:, cols], op0=ALU.mult, op1=ALU.mult,
            )
            if i > 0:
                sign_and_move(*pieces[i - 1])
        sign_and_move(*pieces[-1])

        y_banks = [z2_banks, z1_banks, z2_banks]
        hh_grouped = [grouped_tile("hh%d" % c, width) for c, width in enumerate(widths)]
        result = [
            [sb.tile([P, len(pair), width], F32, name="result%d_%d" % (c, pair[0])) for pair in GROUP_PAIRS]
            for c, width in enumerate(widths)
        ]
        out_rows = out.rearrange("g o n -> o g n")

        def second_layer(c):
            hh_mx = quantize("hh%d" % c, hh_grouped[c], widths[c])
            for pair in GROUP_PAIRS:
                product(y_banks[c], CHUNKS[c], wo_mx, hh_mx, pair)

        def add_residual(c, some_groups):
            cols = CHUNKS[c]
            for g in some_groups:
                pair_result = result[c][g // 2]
                nc.vector.tensor_tensor(
                    out=pair_result[:, g % 2, :], in0=y_banks[c][g][:, cols], in1=res_sb[:, g, cols], op=ALU.add
                )
                if g % 2 == 1:
                    nc.sync.dma_start(out=out_rows[:, g - 1 : g + 1, cols], in_=pair_result[:])

        interleave(nc.scalar.copy, hh_grouped[0], hh_raw[0], slice(0, SCALAR_COLS))
        interleave(nc.vector.tensor_copy, hh_grouped[0], hh_raw[0], slice(SCALAR_COLS, widths[0]))
        second_layer(0)
        interleave(nc.scalar.copy, hh_grouped[1], hh_raw[1], slice(0, widths[1]))
        interleave(nc.scalar.copy, hh_grouped[2], hh_raw[2], slice(0, widths[2]))
        add_residual(0, range(0, 1))
        second_layer(1)
        add_residual(0, range(1, G))
        second_layer(2)
        add_residual(1, groups)
        add_residual(2, groups)
